import numpy as np
import ml_dtypes


def mxq(x, axis, fmt="e4m3"):
    dtype, down = {"e4m3": (ml_dtypes.float8_e4m3fn, 7), "e5m2": (ml_dtypes.float8_e5m2, 14)}[fmt]
    v = np.moveaxis(np.asarray(x, np.float32).astype(ml_dtypes.bfloat16).astype(np.float64), axis, -1)
    blocks = v.reshape(v.shape[:-1] + (-1, 32))
    amax = np.abs(blocks).max(-1, keepdims=True)
    byte = np.maximum(np.where(amax > 0, np.frexp(amax)[1] - 1 + 127, 0) - down, 1)
    scale = np.exp2(byte - 127.0)
    codes = (blocks / scale).astype(np.float32).astype(dtype).astype(np.float64)
    return np.moveaxis((codes * scale).reshape(v.shape), -1, axis)


WIDE = False


def mx_kscale(k):
    if not WIDE:
        return np.ones(k)
    levels = np.array([10, -10, 5, -5, 0])
    if k % 512:
        return np.exp2(np.random.permutation(np.resize(levels, k // 32))).repeat(32)
    a = np.empty((k // 512, 16))
    for p in range(k // 512):
        a[p, :8] = np.random.permutation(np.resize(levels, 8))
        for g in range(8):
            far = levels[np.abs(levels - a[p, g]) >= 10]
            a[p, g + 8] = far[np.random.randint(len(far))]
    return np.exp2(a.ravel()).repeat(32)


BF16 = ml_dtypes.bfloat16


def bf(x):
    return np.asarray(x, np.float32).astype(BF16)


def f64(x):
    return np.asarray(x).astype(np.float64)


E2M1 = np.array([0.0, 0.5, 1.0, 1.5, 2.0, 3.0, 4.0, 6.0, -0.0, -0.5, -1.0, -1.5, -2.0, -3.0, -4.0, -6.0])


def pack_weight(w, fmt):
    k, n = w.shape
    w = f64(bf(w)).reshape(k // 32, 32, n)
    amax = np.abs(w).max(1)
    if fmt == "e4m3":
        byte = np.frexp(amax)[1] - 1 + 127 - 7
    else:
        mant, ex = np.frexp(amax / 6.0)
        byte = np.where(mant > 0.5, ex, ex - 1) + 127
    byte = np.clip(np.where(amax > 0, byte, 1), 1, 254)
    scaled = (w * np.exp2(127.0 - byte)[:, None, :]).reshape(k, n).astype(np.float32)
    by_word = np.ascontiguousarray(scaled.reshape(k // 512, 128, 4, n).transpose(0, 1, 3, 2))
    if fmt == "e4m3":
        words = by_word.astype(ml_dtypes.float8_e4m3fn).view(np.uint8)
    else:
        c = by_word.astype(ml_dtypes.float4_e2m1fn).view(np.uint8) & 0xF
        words = c[..., 0::2] | (c[..., 1::2] << 4)
    return np.ascontiguousarray(words), np.ascontiguousarray(byte.astype(np.uint8).reshape(k // 512, 16, n))


def unpack_weight(words, scales, fmt):
    g, p, n, _ = words.shape
    if fmt == "e4m3":
        vals = np.ascontiguousarray(words).view(ml_dtypes.float8_e4m3fn).astype(np.float64)
    else:
        nib = np.empty((g, p, n, 4), np.uint8)
        nib[..., 0::2] = words & 0xF
        nib[..., 1::2] = words >> 4
        vals = E2M1[nib]
    vals = vals * np.repeat(np.exp2(scales.astype(np.float64) - 127.0), 8, axis=1)[..., None]
    return vals.transpose(0, 1, 3, 2).reshape(g * 512, n)
def pack4(w):
    words, scales = pack_weight(w, "e2m1")
    return words.reshape(words.shape[0], 128, -1), scales


def unpack4(words, scales):
    return unpack_weight(words.reshape(words.shape[0], 128, -1, 2), scales, "e2m1")


E4M3FN = np.array([(-1.0 if i & 128 else 1.0) * ((1.0 + (i & 7) / 8.0) * 2.0 ** (((i >> 3) & 15) - 7) if i & 120 else (i & 7) * 2.0 ** -9) for i in range(256)])


def e4m3fn_bytes(y):
    return np.clip(np.asarray(y, np.float64), -448.0, 448.0).astype(np.float32).astype(ml_dtypes.float8_e4m3fn).view(np.uint8)


def e4m3fn_values(b):
    return E4M3FN[b]


R, K, F, N, B = 1024, 2048, 1024, 1536, 128


def setup_inputs():
    s, t = mx_kscale(K), mx_kscale(F)
    x = np.random.standard_normal((R, K)) * s
    x_scale = (np.abs(x).reshape(R, K // B, B).max(axis=2) / 448.0).astype(np.float32)
    x_bytes = e4m3fn_bytes(x / np.repeat(f64(x_scale), B, axis=1))
    w1 = np.random.standard_normal((K, F)) / np.sqrt(K) / s[:, None] * t
    b1 = 0.4 * np.random.standard_normal(F) * t
    w2 = 2.0 * np.random.standard_normal((F, N)) / np.sqrt(F) / t[:, None]
    b2 = 0.5 * np.random.standard_normal(N)
    w2_words, w2_scales = pack4(w2)
    return {"x_bytes": x_bytes, "x_scale": x_scale,
            "w1": bf(w1), "b1": bf(b1),
            "w2_words": w2_words, "w2_scales": w2_scales, "b2": bf(b2)}


def reference(x_bytes, x_scale, w1, b1, w2_words, w2_scales, b2):
    x = e4m3fn_values(x_bytes) * np.repeat(f64(x_scale), B, axis=1)
    a = mxq(x, 1, "e4m3") @ mxq(f64(w1), 0, "e4m3")
    h = np.maximum(a + f64(b1), 0.0)
    z = (mxq(h, 1, "e4m3") @ unpack4(w2_words, w2_scales)) + f64(b2)
    return 1.0 / (1.0 + np.exp(-z))

@@ -1,0 +1,351 @@
+from contextlib import ExitStack
+
+import concourse.mybir as mybir
+from concourse.masks import make_identity
+
+R, K, F, N = 1024, 2048, 1024, 1536
+FLOPS = 2 * R * K * F + 2 * R * F * N
+
+F32 = mybir.dt.float32
+BF16 = mybir.dt.bfloat16
+I32 = mybir.dt.int32
+U32 = mybir.dt.uint32
+U8 = mybir.dt.uint8
+F8 = mybir.dt.float8_e4m3fn
+FP8X4 = mybir.dt.float8_e4m3fn_x4
+FP4X4 = mybir.dt.float4_e2m1fn_x4
+ACT = mybir.ActivationFunctionType
+ALU = mybir.AluOpType
+
+P = 128
+HALF = 512
+RT = 4
+PASSES = 4
+GROUPS = 2
+CB = 3
+
+
+def tile_radiance_light_colours_d4_kernel(
+    tc, x_bytes, x_scale, w1, b1, w2_words, w2_scales, b2, out
+):
+    nc = tc.nc
+    with ExitStack() as ctx:
+        keep = ctx.enter_context(tc.tile_pool(name="keep", bufs=1))
+        flow = ctx.enter_context(tc.tile_pool(name="flow", bufs=3))
+        psum = ctx.enter_context(tc.psum_pool(name="psum", bufs=1))
+        ctx.enter_context(tc.manual_schedule())
+
+        warm = keep.tile([P, 1], F32, name="warm")
+        nc.vector.memset(warm[:], 0.0)
+        x_sc = keep.tile([P, 8 * 16], F32, name="x_sc")
+        nc.scalar.dma_start(
+            out=x_sc[:].rearrange("p (r b) -> p r b", b=16),
+            in_=x_scale.rearrange("(r p) b -> p r b", p=P),
+        )
+        b1_bf = keep.tile([P, GROUPS, 4], BF16, name="b1_bf")
+        warm_out = keep.tile([P, 1], F32, name="warm_out")
+        nc.scalar.activation(out=warm_out[:], in_=warm[:], func=ACT.Sigmoid)
+        ident = keep.tile([P, P], F32, name="ident")
+        make_identity(nc, ident[:])
+
+        xb = {}
+        wr = {}
+
+        def load_x(h, g):
+            t = keep.tile([P, RT, 512], U8, name=f"x_raw_{h}_{g}")
+            nc.sync.dma_start(
+                out=t[:],
+                in_=x_bytes[HALF * h : HALF * (h + 1), 512 * g : 512 * (g + 1)].rearrange(
+                    "(r p) k -> p r k", p=P
+                ),
+            )
+            xb[h, g] = t
+
+        def load_w(c, g):
+            t = keep.tile([P, 4, 512], BF16, name=f"w_raw_{c}_{g}", align_bytes=64)
+            nc.sync.dma_start(
+                out=t[:],
+                in_=w1[512 * g : 512 * (g + 1), 512 * c : 512 * (c + 1)].rearrange(
+                    "(p j) n -> p j n", j=4
+                ),
+            )
+            wr[c, g] = t
+
+        for g in range(PASSES):
+            load_x(0, g)
+            load_w(0, g)
+        nc.scalar.dma_start(out=b1_bf[:], in_=b1.rearrange("(g p t) -> p g t", p=P, t=4))
+        load_w(1, 0)
+        for g in range(PASSES):
+            if g + 1 < PASSES:
+                load_w(1, g + 1)
+            load_x(1, g)
+        w2_codes = keep.tile([P, GROUPS, 2 * N], U8, name="w2_codes", align_bytes=64)
+        w2_sc = keep.tile([P, GROUPS, N], U8, name="w2_sc", align_bytes=64)
+        nc.gpsimd.memset(w2_sc[:].rearrange("p g n -> p (g n)").bitcast(I32), 0)
+        b2_all = keep.tile([P, N], BF16, name="b2_all")
+        for c in range(GROUPS):
+            nc.sync.dma_start(out=w2_codes[:, c, :].bitcast(I32), in_=w2_words[c].bitcast(I32))
+        for q in range(4):
+            for c in range(GROUPS):
+                nc.sync.dma_start(
+                    out=w2_sc[32 * q : 32 * q + 4, c, :].bitcast(I32),
+                    in_=w2_scales[c, 4 * q : 4 * q + 4, :].bitcast(I32),
+                )
+        nc.sync.dma_start(out=b2_all[:], in_=b2.partition_broadcast(P))
+
+        b1_col = keep.tile([P, GROUPS * 4], F32, name="b1_col")
+
+        xs, tr, xg, xq, xqs, wg, wq, wqs = {}, {}, {}, {}, {}, {}, {}, {}
+
+        def widen(h, g, nv):
+            t = flow.tile([P, RT, 512], BF16, name="x_wide", bufs=4, align_bytes=64)
+            for r in range(RT):
+                for b in range(4):
+                    col = 16 * (RT * h + r) + 4 * g + b
+                    dst = t[:, r, 128 * b : 128 * (b + 1)]
+                    src = xb[h, g][:, r, 128 * b : 128 * (b + 1)].bitcast(F8)
+                    if b < nv // 4 + (r < nv % 4):
+                        nc.vector.tensor_scalar(
+                            out=dst, in0=src, scalar1=x_sc[:, col : col + 1], scalar2=None, op0=ALU.mult
+                        )
+                    else:
+                        nc.scalar.activation(out=dst, in_=src, func=ACT.Copy, scale=x_sc[:, col : col + 1])
+            xs[h, g] = t
+
+        def turn(h, g):
+            words = xs[h, g][:].rearrange("p r k -> p (r k)").bitcast(F32)
+            banks = []
+            for half in range(2):
+                bank = psum.tile([P, 2, 2, P], F32, name="turned", bufs=2)
+                for a in range(2):
+                    for u in range(2):
+                        base = 256 * (2 * half + a)
+                        nc.tensor.transpose(bank[:, a, u, :], words[:, base + u : base + 256 : 2], ident[:])
+                banks.append(bank)
+            tr[h, g] = banks
+
+        def empty(h, g):
+            t = flow.tile([P, HALF * 4], BF16, name="x_grouped", bufs=4, align_bytes=64)
+            view = t[:].bitcast(F32).rearrange("p (a r u) -> p a r u", a=RT, u=2)
+            for half in range(2):
+                nc.scalar.copy(
+                    out=view[:, 2 * half : 2 * half + 2],
+                    in_=tr[h, g][half][:].rearrange("p a u r -> p a r u"),
+                )
+            xg[h, g] = t
+
+        def quant_x(h, g):
+            codes = keep.tile([P, HALF], U32, name=f"x_codes_{h}_{g}", align_bytes=64)
+            sc = keep.tile([P, HALF], U8, name=f"x_qsc_{h}_{g}", align_bytes=64)
+            nc.vector.quantize_mx(out=codes[:].bitcast(FP8X4), scales=sc[:], in_=xg[h, g][:])
+            xq[h, g], xqs[h, g] = codes, sc
+
+        def group_w(c, g, scalar=False):
+            t = flow.tile([P, HALF * 4], BF16, name="w_grouped", bufs=4, align_bytes=64)
+            dst = t[:].rearrange("p (t m j) -> p t m j", t=4, j=4)
+            src = wr[c, g][:].rearrange("p j (m t) -> p t m j", t=4)
+            if scalar:
+                nc.scalar.copy(out=dst, in_=src)
+            else:
+                nc.vector.tensor_copy(out=dst, in_=src)
+            wg[c, g] = t
+
+        def quant_w(c, g):
+            codes = keep.tile([P, HALF], U32, name=f"w_codes_{c}_{g}", align_bytes=64)
+            sc = keep.tile([P, HALF], U8, name=f"w_qsc_{c}_{g}", align_bytes=64)
+            nc.vector.quantize_mx(out=codes[:].bitcast(FP8X4), scales=sc[:], in_=wg[c, g][:])
+            wq[c, g], wqs[c, g] = codes, sc
+
+        acc = {}
+
+        def mm1(c, h, g, ts=(0, 1, 2, 3)):
+            for t in ts:
+                if g == 0:
+                    acc[c, h, t] = psum.tile([P, HALF], F32, name="acc", bufs=6)
+                cols = slice(P * t, P * (t + 1))
+                nc.tensor.matmul_mx(
+                    out=acc[c, h, t][:],
+                    lhsT=wq[c, g][:, cols].bitcast(FP8X4),
+                    lhsT_scale=wqs[c, g][:, cols],
+                    rhs=xq[h, g][:].bitcast(FP8X4),
+                    rhs_scale=xqs[h, g][:],
+                    start=(g == 0),
+                    stop=(g == PASSES - 1),
+                )
+
+        hp, hg, hq, hqs = {}, {}, {}, {}
+
+        def relu(c, h, *ts):
+            for t in ts:
+                if t == 0:
+                    hp[c, h] = flow.tile([P, 4, HALF], BF16, name="h_planes", bufs=2, align_bytes=64)
+                nc.scalar.activation(
+                    out=hp[c, h][:, t, :],
+                    in_=acc[c, h, t][:],
+                    func=ACT.Relu,
+                    bias=b1_col[:, 4 * c + t : 4 * c + t + 1],
+                )
+
+        def group_h(c, h, half):
+            if half == 0:
+                hg[c, h] = flow.tile([P, HALF * 4], BF16, name="h_grouped", bufs=2, align_bytes=64)
+            rays = slice(256 * half, 256 * (half + 1))
+            nc.vector.tensor_copy(
+                out=hg[c, h][:, 1024 * half : 1024 * (half + 1)].rearrange("p (n t) -> p n t", t=4),
+                in_=hp[c, h][:, :, rays].rearrange("p t n -> p n t"),
+            )
+
+        def quant_h(c, h, half):
+            if half == 0:
+                hq[c, h] = keep.tile([P, HALF], U32, name=f"h_codes_{c}_{h}", align_bytes=64)
+                hqs[c, h] = keep.tile([P, HALF], U8, name=f"h_qsc_{c}_{h}", align_bytes=64)
+            rays = slice(256 * half, 256 * (half + 1))
+            nc.vector.quantize_mx(
+                out=hq[c, h][:, rays].bitcast(FP8X4),
+                scales=hqs[c, h][:, rays],
+                in_=hg[c, h][:, 1024 * half : 1024 * (half + 1)],
+            )
+
+        acc2, z, o = {}, {}, {}
+
+        def mm2(h, r):
+            rays = slice(P * r, P * (r + 1))
+            for cb in range(CB):
+                a = psum.tile([P, HALF], F32, name="acc", bufs=6)
+                acc2[h, r, cb] = a
+                for c in range(GROUPS):
+                    nc.tensor.matmul_mx(
+                        out=a[:],
+                        lhsT=hq[c, h][:, rays].bitcast(FP8X4),
+                        lhsT_scale=hqs[c, h][:, rays],
+                        rhs=w2_codes[:, c, 1024 * cb : 1024 * (cb + 1)].bitcast(FP4X4),
+                        rhs_scale=w2_sc[:, c, 512 * cb : 512 * (cb + 1)],
+                        start=(c == 0),
+                        stop=(c == GROUPS - 1),
+                    )
+
+        def bias(h, r, cb):
+            zt = flow.tile([P, 512], F32, name="z", bufs=6)
+            z[h, r, cb] = zt
+            nc.vector.tensor_tensor(
+                out=zt[:], in0=acc2[h, r, cb][:], in1=b2_all[:, 512 * cb : 512 * (cb + 1)], op=ALU.add
+            )
+
+        def sigm(h, r, cb):
+            if cb == 0:
+                o[h, r] = flow.tile([P, N], F32, name="o", bufs=4)
+            nc.scalar.activation(
+                out=o[h, r][:, 512 * cb : 512 * (cb + 1)], in_=z[h, r, cb][:], func=ACT.Sigmoid
+            )
+            row = HALF * h + P * r
+            nc.sync.dma_start(
+                out=out[row : row + P, 512 * cb : 512 * (cb + 1)],
+                in_=o[h, r][:, 512 * cb : 512 * (cb + 1)],
+            )
+
+        def finish(h, r):
+            for cb in range(CB):
+                bias(h, r, cb)
+                sigm(h, r, cb)
+
+        widen(0, 0, 12)
+        turn(0, 0)
+        group_w(0, 0)
+        empty(0, 0)
+        widen(0, 1, 4)
+        turn(0, 1)
+        quant_w(0, 0)
+        group_w(0, 1)
+        quant_x(0, 0)
+        nc.vector.tensor_copy(out=b1_col[:], in_=b1_bf[:].rearrange("p g t -> p (g t)"))
+        for g in range(PASSES):
+            if g + 2 < PASSES:
+                widen(0, g + 2, 4)
+            if g + 1 < PASSES:
+                empty(0, g + 1)
+            mm1(0, 0, g)
+            if g + 2 < PASSES:
+                turn(0, g + 2)
+            if g + 1 < PASSES:
+                quant_w(0, g + 1)
+                if g + 2 < PASSES:
+                    group_w(0, g + 2)
+                else:
+                    group_w(1, 0)
+                quant_x(0, g + 1)
+
+        widen(1, 0, 6)
+        group_w(1, 1)
+        quant_w(1, 0)
+        relu(0, 0, 0, 1)
+        turn(1, 0)
+        mm1(1, 0, 0)
+        widen(1, 1, 6)
+        empty(1, 0)
+        relu(0, 0, 2, 3)
+        group_w(1, 2)
+        quant_w(1, 1)
+        quant_x(1, 0)
+        turn(1, 1)
+        mm1(1, 0, 1)
+        mm1(0, 1, 0, ts=(0, 1))
+        widen(1, 2, 6)
+        empty(1, 1)
+        group_h(0, 0, 0)
+        group_h(0, 0, 1)
+        quant_w(1, 2)
+        group_w(1, 3)
+        quant_x(1, 1)
+        quant_h(0, 0, 0)
+        quant_h(0, 0, 1)
+        turn(1, 2)
+        mm1(1, 0, 2)
+        mm1(0, 1, 1, ts=(0, 1))
+        widen(1, 3, 6)
+        empty(1, 2)
+        quant_w(1, 3)
+        quant_x(1, 2)
+        turn(1, 3)
+        mm1(1, 0, 3)
+        mm1(0, 1, 2, ts=(0, 1))
+        empty(1, 3)
+        relu(1, 0, 0, 1, 2, 3)
+        quant_x(1, 3)
+        mm1(0, 1, 3, ts=(0, 1))
+        for t in (2, 3):
+            for g in range(PASSES):
+                mm1(0, 1, g, ts=(t,))
+        group_h(1, 0, 0)
+        group_h(1, 0, 1)
+        quant_h(1, 0, 0)
+        quant_h(1, 0, 1)
+        relu(0, 1, 0, 1, 2, 3)
+        for t in (0, 1):
+            for g in range(PASSES):
+                mm1(1, 1, g, ts=(t,))
+        mm2(0, 0)
+        finish(0, 0)
+        relu(1, 1, 0)
+        mm2(0, 1)
+        group_h(0, 1, 0)
+        group_h(0, 1, 1)
+        finish(0, 1)
+        quant_h(0, 1, 0)
+        quant_h(0, 1, 1)
+        relu(1, 1, 1)
+        for t in (2, 3):
+            for g in range(PASSES):
+                mm1(1, 1, g, ts=(t,))
+        relu(1, 1, 2, 3)
+        mm2(0, 2)
+        finish(0, 2)
+        group_h(1, 1, 0)
+        group_h(1, 1, 1)
+        quant_h(1, 1, 0)
+        quant_h(1, 1, 1)
+        mm2(0, 3)
+        finish(0, 3)
+        for r in range(RT):
+            mm2(1, r)
+            finish(1, r)

@@ -143,8 +143,8 @@ def tile_radiance_light_colours_d4_kernel(
 
         def group_w(c, g, scalar=False):
             t = flow.tile([P, HALF * 4], BF16, name="w_grouped", bufs=4, align_bytes=64)
-            dst = t[:].rearrange("p (t m j) -> p t m j", t=4, j=4)
-            src = wr[c, g][:].rearrange("p j (m t) -> p t m j", t=4)
+            dst = t[:].rearrange("p (t m j) -> p m j t", t=4, j=4)
+            src = wr[c, g][:].rearrange("p j (m t) -> p m j t", t=4)
             if scalar:
                 nc.scalar.copy(out=dst, in_=src)
             else:
@@ -192,8 +192,8 @@ def tile_radiance_light_colours_d4_kernel(
                 hg[c, h] = flow.tile([P, HALF * 4], BF16, name="h_grouped", bufs=2, align_bytes=64)
             rays = slice(256 * half, 256 * (half + 1))
             nc.vector.tensor_copy(
-                out=hg[c, h][:, 1024 * half : 1024 * (half + 1)].rearrange("p (n t) -> p n t", t=4),
-                in_=hp[c, h][:, :, rays].rearrange("p t n -> p n t"),
+                out=hg[c, h][:, 1024 * half : 1024 * (half + 1)].rearrange("p (n i t) -> p n t i", i=4, t=4),
+                in_=hp[c, h][:, :, rays].rearrange("p t (n i) -> p n t i", i=4),
             )
 
         def quant_h(c, h, half):

@@ -39,8 +39,8 @@ def tile_radiance_light_colours_d4_kernel(
         nc.vector.memset(warm[:], 0.0)
         x_sc = keep.tile([P, 8 * 16], F32, name="x_sc")
         nc.scalar.dma_start(
-            out=x_sc[:].rearrange("p (r b) -> p r b", b=16),
-            in_=x_scale.rearrange("(r p) b -> p r b", p=P),
+            out=x_sc[:],
+            in_=x_scale.rearrange("(p r) b -> p (r b)", p=P),
         )
         b1_bf = keep.tile([P, GROUPS, 4], BF16, name="b1_bf")
         warm_out = keep.tile([P, 1], F32, name="warm_out")
@@ -51,15 +51,16 @@ def tile_radiance_light_colours_d4_kernel(
         xb = {}
         wr = {}
 
-        def load_x(h, g):
-            t = keep.tile([P, RT, 512], U8, name=f"x_raw_{h}_{g}")
+        x_rows = x_bytes.rearrange("(p r) k -> p r k", p=P)
+        out_rows = out.rearrange("(p r) n -> p r n", p=P)
+
+        def load_x(h, g, passes):
+            t = keep.tile([P, RT, 512 * passes], U8, name=f"x_raw_{h}_{g}")
             nc.sync.dma_start(
-                out=t[:],
-                in_=x_bytes[HALF * h : HALF * (h + 1), 512 * g : 512 * (g + 1)].rearrange(
-                    "(r p) k -> p r k", p=P
-                ),
+                out=t[:], in_=x_rows[:, RT * h : RT * (h + 1), 512 * g : 512 * (g + passes)]
             )
-            xb[h, g] = t
+            for i in range(passes):
+                xb[h, g + i] = t[:, :, 512 * i : 512 * (i + 1)]
 
         def load_w(c, g):
             t = keep.tile([P, 4, 512], BF16, name=f"w_raw_{c}_{g}", align_bytes=64)
@@ -71,15 +72,20 @@ def tile_radiance_light_colours_d4_kernel(
             )
             wr[c, g] = t
 
-        for g in range(PASSES):
-            load_x(0, g)
-            load_w(0, g)
+        load_x(0, 0, 1)
+        load_w(0, 0)
+        load_x(0, 1, 1)
+        load_w(0, 1)
         nc.scalar.dma_start(out=b1_bf[:], in_=b1.rearrange("(g p t) -> p g t", p=P, t=4))
+        load_x(0, 2, 2)
+        load_w(0, 2)
+        load_w(0, 3)
         load_w(1, 0)
-        for g in range(PASSES):
-            if g + 1 < PASSES:
-                load_w(1, g + 1)
-            load_x(1, g)
+        load_w(1, 1)
+        load_x(1, 0, 2)
+        load_w(1, 2)
+        load_x(1, 2, 2)
+        load_w(1, 3)
         w2_codes = keep.tile([P, GROUPS, 2 * N], U8, name="w2_codes", align_bytes=64)
         w2_sc = keep.tile([P, GROUPS, N], U8, name="w2_sc", align_bytes=64)
         nc.gpsimd.memset(w2_sc[:].rearrange("p g n -> p (g n)").bitcast(I32), 0)
@@ -98,30 +104,41 @@ def tile_radiance_light_colours_d4_kernel(
 
         xs, tr, xg, xq, xqs, wg, wq, wqs = {}, {}, {}, {}, {}, {}, {}, {}
 
+        on_vector = {}
+
         def widen(h, g, nv):
             t = flow.tile([P, RT, 512], BF16, name="x_wide", bufs=4, align_bytes=64)
             for r in range(RT):
                 for b in range(4):
                     col = 16 * (RT * h + r) + 4 * g + b
-                    dst = t[:, r, 128 * b : 128 * (b + 1)]
+                    sc = x_sc[:, col : col + 1]
                     src = xb[h, g][:, r, 128 * b : 128 * (b + 1)].bitcast(F8)
-                    if b < nv // 4 + (r < nv % 4):
+                    if r < nv:
+                        dst = t[:, r, :].rearrange("p (u a e) -> p a u e", u=2, e=2)[:, 32 * b : 32 * (b + 1)]
                         nc.vector.tensor_scalar(
-                            out=dst, in0=src, scalar1=x_sc[:, col : col + 1], scalar2=None, op0=ALU.mult
+                            out=dst,
+                            in0=src.rearrange("p (a u e) -> p a u e", u=2, e=2),
+                            scalar1=sc,
+                            scalar2=None,
+                            op0=ALU.mult,
                         )
                     else:
-                        nc.scalar.activation(out=dst, in_=src, func=ACT.Copy, scale=x_sc[:, col : col + 1])
+                        dst = t[:, r, 128 * b : 128 * (b + 1)]
+                        nc.scalar.activation(out=dst, in_=src, func=ACT.Copy, scale=sc)
             xs[h, g] = t
+            on_vector[h, g] = nv
 
         def turn(h, g):
             words = xs[h, g][:].rearrange("p r k -> p (r k)").bitcast(F32)
             banks = []
             for half in range(2):
-                bank = psum.tile([P, 2, 2, P], F32, name="turned", bufs=2)
+                bank = psum.tile([P, 2, 2, P], F32, name="turned", tag="bank", bufs=8)
                 for a in range(2):
                     for u in range(2):
-                        base = 256 * (2 * half + a)
-                        nc.tensor.transpose(bank[:, a, u, :], words[:, base + u : base + 256 : 2], ident[:])
+                        r = 2 * half + a
+                        w = words[:, 256 * r : 256 * (r + 1)]
+                        w = w[:, P * u : P * (u + 1)] if r < on_vector[h, g] else w[:, u::2]
+                        nc.tensor.transpose(bank[:, a, u, :], w, ident[:])
                 banks.append(bank)
             tr[h, g] = banks
 
@@ -162,7 +179,7 @@ def tile_radiance_light_colours_d4_kernel(
         def mm1(c, h, g, ts=(0, 1, 2, 3)):
             for t in ts:
                 if g == 0:
-                    acc[c, h, t] = psum.tile([P, HALF], F32, name="acc", bufs=6)
+                    acc[c, h, t] = psum.tile([P, HALF], F32, name="acc", tag="bank", bufs=8)
                 cols = slice(P * t, P * (t + 1))
                 nc.tensor.matmul_mx(
                     out=acc[c, h, t][:],
@@ -212,7 +229,7 @@ def tile_radiance_light_colours_d4_kernel(
         def mm2(h, r):
             rays = slice(P * r, P * (r + 1))
             for cb in range(CB):
-                a = psum.tile([P, HALF], F32, name="acc", bufs=6)
+                a = psum.tile([P, HALF], F32, name="acc2", tag="bank", bufs=8)
                 acc2[h, r, cb] = a
                 for c in range(GROUPS):
                     nc.tensor.matmul_mx(
@@ -238,22 +255,22 @@ def tile_radiance_light_colours_d4_kernel(
             nc.scalar.activation(
                 out=o[h, r][:, 512 * cb : 512 * (cb + 1)], in_=z[h, r, cb][:], func=ACT.Sigmoid
             )
-            row = HALF * h + P * r
-            nc.sync.dma_start(
-                out=out[row : row + P, 512 * cb : 512 * (cb + 1)],
-                in_=o[h, r][:, 512 * cb : 512 * (cb + 1)],
-            )
+            if h == 1 or r >= 2:
+                cols = slice(512 * cb, 512 * (cb + 1))
+                nc.sync.dma_start(out=out_rows[:, RT * h + r, cols], in_=o[h, r][:, cols])
+            elif cb == CB - 1:
+                nc.sync.dma_start(out=out_rows[:, r, :], in_=o[h, r][:])
 
         def finish(h, r):
             for cb in range(CB):
                 bias(h, r, cb)
                 sigm(h, r, cb)
 
-        widen(0, 0, 12)
+        widen(0, 0, 3)
         turn(0, 0)
         group_w(0, 0)
         empty(0, 0)
-        widen(0, 1, 4)
+        widen(0, 1, 1)
         turn(0, 1)
         quant_w(0, 0)
         group_w(0, 1)
@@ -261,7 +278,7 @@ def tile_radiance_light_colours_d4_kernel(
         nc.vector.tensor_copy(out=b1_col[:], in_=b1_bf[:].rearrange("p g t -> p (g t)"))
         for g in range(PASSES):
             if g + 2 < PASSES:
-                widen(0, g + 2, 4)
+                widen(0, g + 2, 1)
             if g + 1 < PASSES:
                 empty(0, g + 1)
             mm1(0, 0, g)
@@ -271,17 +288,16 @@ def tile_radiance_light_colours_d4_kernel(
                 quant_w(0, g + 1)
                 if g + 2 < PASSES:
                     group_w(0, g + 2)
-                else:
-                    group_w(1, 0)
                 quant_x(0, g + 1)
+        group_w(1, 0)
 
-        widen(1, 0, 6)
+        widen(1, 0, 1)
         group_w(1, 1)
         quant_w(1, 0)
         relu(0, 0, 0, 1)
         turn(1, 0)
         mm1(1, 0, 0)
-        widen(1, 1, 6)
+        widen(1, 1, 1)
         empty(1, 0)
         relu(0, 0, 2, 3)
         group_w(1, 2)
@@ -290,43 +306,46 @@ def tile_radiance_light_colours_d4_kernel(
         turn(1, 1)
         mm1(1, 0, 1)
         mm1(0, 1, 0, ts=(0, 1))
-        widen(1, 2, 6)
+        widen(1, 2, 2)
         empty(1, 1)
         group_h(0, 0, 0)
         group_h(0, 0, 1)
         quant_w(1, 2)
         group_w(1, 3)
         quant_x(1, 1)
-        quant_h(0, 0, 0)
-        quant_h(0, 0, 1)
         turn(1, 2)
         mm1(1, 0, 2)
-        mm1(0, 1, 1, ts=(0, 1))
-        widen(1, 3, 6)
+        widen(1, 3, 2)
+        quant_h(0, 0, 0)
+        quant_h(0, 0, 1)
         empty(1, 2)
+        turn(1, 3)
+        mm1(0, 1, 1, ts=(0, 1))
         quant_w(1, 3)
         quant_x(1, 2)
-        turn(1, 3)
         mm1(1, 0, 3)
-        mm1(0, 1, 2, ts=(0, 1))
         empty(1, 3)
+        mm1(0, 1, 2, ts=(0, 1))
         relu(1, 0, 0, 1, 2, 3)
         quant_x(1, 3)
         mm1(0, 1, 3, ts=(0, 1))
         for t in (2, 3):
             for g in range(PASSES):
                 mm1(0, 1, g, ts=(t,))
+        relu(0, 1, 0, 1)
         group_h(1, 0, 0)
         group_h(1, 0, 1)
         quant_h(1, 0, 0)
         quant_h(1, 0, 1)
-        relu(0, 1, 0, 1, 2, 3)
+        relu(0, 1, 2, 3)
         for t in (0, 1):
             for g in range(PASSES):
                 mm1(1, 1, g, ts=(t,))
         mm2(0, 0)
         finish(0, 0)
         relu(1, 1, 0)
+        for g in range(PASSES):
+            mm1(1, 1, g, ts=(2,))
         mm2(0, 1)
         group_h(0, 1, 0)
         group_h(0, 1, 1)
@@ -334,9 +353,8 @@ def tile_radiance_light_colours_d4_kernel(
         quant_h(0, 1, 0)
         quant_h(0, 1, 1)
         relu(1, 1, 1)
-        for t in (2, 3):
-            for g in range(PASSES):
-                mm1(1, 1, g, ts=(t,))
+        for g in range(PASSES):
+            mm1(1, 1, g, ts=(3,))
         relu(1, 1, 2, 3)
         mm2(0, 2)
         finish(0, 2)

from contextlib import ExitStack

import concourse.mybir as mybir
from concourse.masks import make_identity

R, K, F, N = 1024, 2048, 1024, 1536
FLOPS = 2 * R * K * F + 2 * R * F * N

F32 = mybir.dt.float32
BF16 = mybir.dt.bfloat16
I32 = mybir.dt.int32
U32 = mybir.dt.uint32
U8 = mybir.dt.uint8
F8 = mybir.dt.float8_e4m3fn
FP8X4 = mybir.dt.float8_e4m3fn_x4
FP4X4 = mybir.dt.float4_e2m1fn_x4
ACT = mybir.ActivationFunctionType
ALU = mybir.AluOpType

P = 128
HALF = 512
RT = 4
PASSES = 4
GROUPS = 2
CB = 3


def tile_radiance_light_colours_d4_kernel(
    tc, x_bytes, x_scale, w1, b1, w2_words, w2_scales, b2, out
):
    nc = tc.nc
    with ExitStack() as ctx:
        keep = ctx.enter_context(tc.tile_pool(name="keep", bufs=1))
        flow = ctx.enter_context(tc.tile_pool(name="flow", bufs=3))
        psum = ctx.enter_context(tc.psum_pool(name="psum", bufs=1))
        ctx.enter_context(tc.manual_schedule())

        warm = keep.tile([P, 1], F32, name="warm")
        nc.vector.memset(warm[:], 0.0)
        x_sc = keep.tile([P, 8 * 16], F32, name="x_sc")
        nc.scalar.dma_start(
            out=x_sc[:],
            in_=x_scale.rearrange("(p r) b -> p (r b)", p=P),
        )
        b1_bf = keep.tile([P, GROUPS, 4], BF16, name="b1_bf")
        warm_out = keep.tile([P, 1], F32, name="warm_out")
        nc.scalar.activation(out=warm_out[:], in_=warm[:], func=ACT.Sigmoid)
        ident = keep.tile([P, P], F32, name="ident")
        make_identity(nc, ident[:])

        xb = {}
        wr = {}

        x_rows = x_bytes.rearrange("(p r) k -> p r k", p=P)
        out_rows = out.rearrange("(p r) n -> p r n", p=P)

        def load_x(h, g, passes):
            t = keep.tile([P, RT, 512 * passes], U8, name=f"x_raw_{h}_{g}")
            nc.sync.dma_start(
                out=t[:], in_=x_rows[:, RT * h : RT * (h + 1), 512 * g : 512 * (g + passes)]
            )
            for i in range(passes):
                xb[h, g + i] = t[:, :, 512 * i : 512 * (i + 1)]

        def load_w(c, g):
            t = keep.tile([P, 4, 512], BF16, name=f"w_raw_{c}_{g}", align_bytes=64)
            nc.sync.dma_start(
                out=t[:],
                in_=w1[512 * g : 512 * (g + 1), 512 * c : 512 * (c + 1)].rearrange(
                    "(p j) n -> p j n", j=4
                ),
            )
            wr[c, g] = t

        load_x(0, 0, 1)
        load_w(0, 0)
        load_x(0, 1, 1)
        load_w(0, 1)
        nc.scalar.dma_start(out=b1_bf[:], in_=b1.rearrange("(g p t) -> p g t", p=P, t=4))
        load_x(0, 2, 2)
        load_w(0, 2)
        load_w(0, 3)
        load_w(1, 0)
        load_w(1, 1)
        load_x(1, 0, 2)
        load_w(1, 2)
        load_x(1, 2, 2)
        load_w(1, 3)
        w2_codes = keep.tile([P, GROUPS, 2 * N], U8, name="w2_codes", align_bytes=64)
        w2_sc = keep.tile([P, GROUPS, N], U8, name="w2_sc", align_bytes=64)
        nc.gpsimd.memset(w2_sc[:].rearrange("p g n -> p (g n)").bitcast(I32), 0)
        b2_all = keep.tile([P, N], BF16, name="b2_all")
        for c in range(GROUPS):
            nc.sync.dma_start(out=w2_codes[:, c, :].bitcast(I32), in_=w2_words[c].bitcast(I32))
        for q in range(4):
            for c in range(GROUPS):
                nc.sync.dma_start(
                    out=w2_sc[32 * q : 32 * q + 4, c, :].bitcast(I32),
                    in_=w2_scales[c, 4 * q : 4 * q + 4, :].bitcast(I32),
                )
        nc.sync.dma_start(out=b2_all[:], in_=b2.partition_broadcast(P))

        b1_col = keep.tile([P, GROUPS * 4], F32, name="b1_col")

        xs, tr, xg, xq, xqs, wg, wq, wqs = {}, {}, {}, {}, {}, {}, {}, {}

        on_vector = {}

        def widen(h, g, nv):
            t = flow.tile([P, RT, 512], BF16, name="x_wide", bufs=4, align_bytes=64)
            for r in range(RT):
                for b in range(4):
                    col = 16 * (RT * h + r) + 4 * g + b
                    sc = x_sc[:, col : col + 1]
                    src = xb[h, g][:, r, 128 * b : 128 * (b + 1)].bitcast(F8)
                    if r < nv:
                        dst = t[:, r, :].rearrange("p (u a e) -> p a u e", u=2, e=2)[:, 32 * b : 32 * (b + 1)]
                        nc.vector.tensor_scalar(
                            out=dst,
                            in0=src.rearrange("p (a u e) -> p a u e", u=2, e=2),
                            scalar1=sc,
                            scalar2=None,
                            op0=ALU.mult,
                        )
                    else:
                        dst = t[:, r, 128 * b : 128 * (b + 1)]
                        nc.scalar.activation(out=dst, in_=src, func=ACT.Copy, scale=sc)
            xs[h, g] = t
            on_vector[h, g] = nv

        def turn(h, g):
            words = xs[h, g][:].rearrange("p r k -> p (r k)").bitcast(F32)
            banks = []
            for half in range(2):
                bank = psum.tile([P, 2, 2, P], F32, name="turned", tag="bank", bufs=8)
                for a in range(2):
                    for u in range(2):
                        r = 2 * half + a
                        w = words[:, 256 * r : 256 * (r + 1)]
                        w = w[:, P * u : P * (u + 1)] if r < on_vector[h, g] else w[:, u::2]
                        nc.tensor.transpose(bank[:, a, u, :], w, ident[:])
                banks.append(bank)
            tr[h, g] = banks

        def empty(h, g):
            t = flow.tile([P, HALF * 4], BF16, name="x_grouped", bufs=4, align_bytes=64)
            view = t[:].bitcast(F32).rearrange("p (a r u) -> p a r u", a=RT, u=2)
            for half in range(2):
                nc.scalar.copy(
                    out=view[:, 2 * half : 2 * half + 2],
                    in_=tr[h, g][half][:].rearrange("p a u r -> p a r u"),
                )
            xg[h, g] = t

        def quant_x(h, g):
            codes = keep.tile([P, HALF], U32, name=f"x_codes_{h}_{g}", align_bytes=64)
            sc = keep.tile([P, HALF], U8, name=f"x_qsc_{h}_{g}", align_bytes=64)
            nc.vector.quantize_mx(out=codes[:].bitcast(FP8X4), scales=sc[:], in_=xg[h, g][:])
            xq[h, g], xqs[h, g] = codes, sc

        def group_w(c, g, scalar=False):
            t = flow.tile([P, HALF * 4], BF16, name="w_grouped", bufs=4, align_bytes=64)
            dst = t[:].rearrange("p (t m j) -> p m j t", t=4, j=4)
            src = wr[c, g][:].rearrange("p j (m t) -> p m j t", t=4)
            if scalar:
                nc.scalar.copy(out=dst, in_=src)
            else:
                nc.vector.tensor_copy(out=dst, in_=src)
            wg[c, g] = t

        def quant_w(c, g):
            codes = keep.tile([P, HALF], U32, name=f"w_codes_{c}_{g}", align_bytes=64)
            sc = keep.tile([P, HALF], U8, name=f"w_qsc_{c}_{g}", align_bytes=64)
            nc.vector.quantize_mx(out=codes[:].bitcast(FP8X4), scales=sc[:], in_=wg[c, g][:])
            wq[c, g], wqs[c, g] = codes, sc

        acc = {}

        def mm1(c, h, g, ts=(0, 1, 2, 3)):
            for t in ts:
                if g == 0:
                    acc[c, h, t] = psum.tile([P, HALF], F32, name="acc", tag="bank", bufs=8)
                cols = slice(P * t, P * (t + 1))
                nc.tensor.matmul_mx(
                    out=acc[c, h, t][:],
                    lhsT=wq[c, g][:, cols].bitcast(FP8X4),
                    lhsT_scale=wqs[c, g][:, cols],
                    rhs=xq[h, g][:].bitcast(FP8X4),
                    rhs_scale=xqs[h, g][:],
                    start=(g == 0),
                    stop=(g == PASSES - 1),
                )

        hp, hg, hq, hqs = {}, {}, {}, {}

        def relu(c, h, *ts):
            for t in ts:
                if t == 0:
                    hp[c, h] = flow.tile([P, 4, HALF], BF16, name="h_planes", bufs=2, align_bytes=64)
                nc.scalar.activation(
                    out=hp[c, h][:, t, :],
                    in_=acc[c, h, t][:],
                    func=ACT.Relu,
                    bias=b1_col[:, 4 * c + t : 4 * c + t + 1],
                )

        def group_h(c, h, half):
            if half == 0:
                hg[c, h] = flow.tile([P, HALF * 4], BF16, name="h_grouped", bufs=2, align_bytes=64)
            rays = slice(256 * half, 256 * (half + 1))
            nc.vector.tensor_copy(
                out=hg[c, h][:, 1024 * half : 1024 * (half + 1)].rearrange("p (n i t) -> p n t i", i=4, t=4),
                in_=hp[c, h][:, :, rays].rearrange("p t (n i) -> p n t i", i=4),
            )

        def quant_h(c, h, half):
            if half == 0:
                hq[c, h] = keep.tile([P, HALF], U32, name=f"h_codes_{c}_{h}", align_bytes=64)
                hqs[c, h] = keep.tile([P, HALF], U8, name=f"h_qsc_{c}_{h}", align_bytes=64)
            rays = slice(256 * half, 256 * (half + 1))
            nc.vector.quantize_mx(
                out=hq[c, h][:, rays].bitcast(FP8X4),
                scales=hqs[c, h][:, rays],
                in_=hg[c, h][:, 1024 * half : 1024 * (half + 1)],
            )

        acc2, z, o = {}, {}, {}

        def mm2(h, r):
            rays = slice(P * r, P * (r + 1))
            for cb in range(CB):
                a = psum.tile([P, HALF], F32, name="acc2", tag="bank", bufs=8)
                acc2[h, r, cb] = a
                for c in range(GROUPS):
                    nc.tensor.matmul_mx(
                        out=a[:],
                        lhsT=hq[c, h][:, rays].bitcast(FP8X4),
                        lhsT_scale=hqs[c, h][:, rays],
                        rhs=w2_codes[:, c, 1024 * cb : 1024 * (cb + 1)].bitcast(FP4X4),
                        rhs_scale=w2_sc[:, c, 512 * cb : 512 * (cb + 1)],
                        start=(c == 0),
                        stop=(c == GROUPS - 1),
                    )

        def bias(h, r, cb):
            zt = flow.tile([P, 512], F32, name="z", bufs=6)
            z[h, r, cb] = zt
            nc.vector.tensor_tensor(
                out=zt[:], in0=acc2[h, r, cb][:], in1=b2_all[:, 512 * cb : 512 * (cb + 1)], op=ALU.add
            )

        def sigm(h, r, cb):
            if cb == 0:
                o[h, r] = flow.tile([P, N], F32, name="o", bufs=4)
            nc.scalar.activation(
                out=o[h, r][:, 512 * cb : 512 * (cb + 1)], in_=z[h, r, cb][:], func=ACT.Sigmoid
            )
            if h == 1 or r >= 2:
                cols = slice(512 * cb, 512 * (cb + 1))
                nc.sync.dma_start(out=out_rows[:, RT * h + r, cols], in_=o[h, r][:, cols])
            elif cb == CB - 1:
                nc.sync.dma_start(out=out_rows[:, r, :], in_=o[h, r][:])

        def finish(h, r):
            for cb in range(CB):
                bias(h, r, cb)
                sigm(h, r, cb)

        widen(0, 0, 3)
        turn(0, 0)
        group_w(0, 0)
        empty(0, 0)
        widen(0, 1, 1)
        turn(0, 1)
        quant_w(0, 0)
        group_w(0, 1)
        quant_x(0, 0)
        nc.vector.tensor_copy(out=b1_col[:], in_=b1_bf[:].rearrange("p g t -> p (g t)"))
        for g in range(PASSES):
            if g + 2 < PASSES:
                widen(0, g + 2, 1)
            if g + 1 < PASSES:
                empty(0, g + 1)
            mm1(0, 0, g)
            if g + 2 < PASSES:
                turn(0, g + 2)
            if g + 1 < PASSES:
                quant_w(0, g + 1)
                if g + 2 < PASSES:
                    group_w(0, g + 2)
                quant_x(0, g + 1)
        group_w(1, 0)

        widen(1, 0, 1)
        group_w(1, 1)
        quant_w(1, 0)
        relu(0, 0, 0, 1)
        turn(1, 0)
        mm1(1, 0, 0)
        widen(1, 1, 1)
        empty(1, 0)
        relu(0, 0, 2, 3)
        group_w(1, 2)
        quant_w(1, 1)
        quant_x(1, 0)
        turn(1, 1)
        mm1(1, 0, 1)
        mm1(0, 1, 0, ts=(0, 1))
        widen(1, 2, 2)
        empty(1, 1)
        group_h(0, 0, 0)
        group_h(0, 0, 1)
        quant_w(1, 2)
        group_w(1, 3)
        quant_x(1, 1)
        turn(1, 2)
        mm1(1, 0, 2)
        widen(1, 3, 2)
        quant_h(0, 0, 0)
        quant_h(0, 0, 1)
        empty(1, 2)
        turn(1, 3)
        mm1(0, 1, 1, ts=(0, 1))
        quant_w(1, 3)
        quant_x(1, 2)
        mm1(1, 0, 3)
        empty(1, 3)
        mm1(0, 1, 2, ts=(0, 1))
        relu(1, 0, 0, 1, 2, 3)
        quant_x(1, 3)
        mm1(0, 1, 3, ts=(0, 1))
        for t in (2, 3):
            for g in range(PASSES):
                mm1(0, 1, g, ts=(t,))
        relu(0, 1, 0, 1)
        group_h(1, 0, 0)
        group_h(1, 0, 1)
        quant_h(1, 0, 0)
        quant_h(1, 0, 1)
        relu(0, 1, 2, 3)
        for t in (0, 1):
            for g in range(PASSES):
                mm1(1, 1, g, ts=(t,))
        mm2(0, 0)
        finish(0, 0)
        relu(1, 1, 0)
        for g in range(PASSES):
            mm1(1, 1, g, ts=(2,))
        mm2(0, 1)
        group_h(0, 1, 0)
        group_h(0, 1, 1)
        finish(0, 1)
        quant_h(0, 1, 0)
        quant_h(0, 1, 1)
        relu(1, 1, 1)
        for g in range(PASSES):
            mm1(1, 1, g, ts=(3,))
        relu(1, 1, 2, 3)
        mm2(0, 2)
        finish(0, 2)
        group_h(1, 1, 0)
        group_h(1, 1, 1)
        quant_h(1, 1, 0)
        quant_h(1, 1, 1)
        mm2(0, 3)
        finish(0, 3)
        for r in range(RT):
            mm2(1, r)
            finish(1, r)
